import numpy as np
CORES = [66,74,82,90,194,202,210,218]
N = 8
CB = 64
def setup_inputs(rng):
    return {"x": rng.standard_normal((N, 128, N * CB), dtype=np.float32)}
def setup_inputs_big(rng):
    d = setup_inputs(rng)
    for k in ("x",): d[k] = (d[k].astype(np.float32) * 1024.0).astype(d[k].dtype)
    return d
def setup_inputs_small(rng):
    d = setup_inputs(rng)
    for k in ("x",): d[k] = (d[k].astype(np.float32) * (1 / 1024.0)).astype(d[k].dtype)
    return d
def setup_inputs_apart(rng):
    d = setup_inputs(rng)
    f = (10.0 ** rng.permutation(np.linspace(-1.5, 1.5, N))).astype(np.float32).reshape(N, 1, 1)
    for k in ("x",): d[k] = (d[k].astype(np.float32) * f).astype(d[k].dtype)
    return d
def reference(x):
    X = x.astype(np.float64)
    G = sum(X[j].T @ X[j] for j in range(N))
    y = np.full((N, CB, N * CB), np.nan)
    for r in range(N):
        y[r][:, :CB * r] = G[CB * r:CB * r + CB, :CB * r]
    return {"y": y.astype(np.float32 if x.dtype != np.float64 else np.float64)}

@@ -1,0 +1,107 @@
+from concourse.mybir import AluOpType
+
+N = 8
+CB = 64
+HALF = CB // 2
+
+
+def _w(r):
+    return HALF * r
+
+
+_OFF = [sum(_w(q) for q in range(r)) for r in range(N + 1)]
+
+SCRATCH = {
+    "xs": ("sbuf", [128, N * CB], "float32"),
+    "snd": ("sbuf", [128, _OFF[N]], "float32"),
+    "land": ("sbuf", [128, (N - 1) * _w(N - 1)], "float32"),
+    "res": ("sbuf", [128, _w(N - 1)], "float32"),
+}
+for _r in range(1, N):
+    SCRATCH["ps%d" % _r] = ("psum", [128, 512], "float32")
+
+SEMAPHORES = (["lda", "ldb", "acc", "sent", "st"]
+              + ["mm%d" % r for r in range(1, N)]
+              + ["ev%d" % r for r in range(1, N)]
+              + ["arr%d" % j for j in range(N)])
+
+_FIRST = {0: 7, 1: 6, 2: 5, 3: 4, 4: 3, 5: 2, 6: 4, 7: 6}
+
+
+def _order(j):
+    dests = [r for r in range(1, N) if r != j]
+    opener = dests[0]
+    ring = list(range(N - 1, 1, -1))
+    k = ring.index(_FIRST[j])
+    ring = ring[k:] + ring[:k]
+    return [opener] + [r for r in ring if r != j and r != opener]
+
+
+def _arrival_order(r):
+    when = {}
+    for j in range(N):
+        if j == r:
+            continue
+        t = 0
+        for d in _order(j):
+            t += 4 + d
+            if d == r:
+                break
+        when[j] = t
+    return sorted(when, key=lambda j: (when[j], j))
+
+
+def rank_program(g, core, T, topo):
+    p = T.rank_of(core)
+    if p is None:
+        return
+    sem = T.sem
+    order = _order(p)
+    ca = CB * (order[0] + 1)
+
+    g.sync.dma_start(T.xs[:, 0:ca], T.x[:, 0:ca]).then_inc(sem.lda, 16)
+    g.scalar.dma_start(T.xs[:, ca:N * CB], T.x[:, ca:N * CB]).then_inc(sem.ldb, 16)
+
+    g.tensor.wait_ge(sem.lda, 16)
+    work = order + ([p] if p >= 1 else [])
+    for i, r in enumerate(work):
+        if i == 1:
+            g.tensor.wait_ge(sem.ldb, 16)
+        w = _w(r)
+        ps = T["ps%d" % r]
+        blk = T.xs[:, CB * r:CB * r + CB]
+        g.tensor.matmul(ps[0:64, 0:w], lhsT=blk, rhs=T.xs[:, 0:w], start=True, stop=True).then_inc(sem["mm%d" % r], 1)
+        g.tensor.matmul(ps[64:128, 0:w], lhsT=blk, rhs=T.xs[:, w:2 * w], start=True, stop=True).then_inc(sem["mm%d" % r], 1)
+
+    sent = 0
+    for r in order:
+        w = _w(r)
+        g.vector.wait_ge(sem["mm%d" % r], 2)
+        g.vector.tensor_copy(T.snd[:, _OFF[r]:_OFF[r] + w], T["ps%d" % r][:, 0:w]).then_inc(sem["ev%d" % r], 1)
+        dst = T.cores[r]
+        rid, pid = topo.addr(dst, core)
+        mask = topo.mask(core, dst)
+        slot = p if p < r else p - 1
+        g.wait_ge(sem["ev%d" % r], 1)
+        g.remote_dma(out_ap=T.land[:, slot * w:(slot + 1) * w], in_ap=T.snd[:, _OFF[r]:_OFF[r] + w],
+                     remote_sem=sem["arr%d" % p], local_sem=sem.sent, pid=pid, routing_id=rid, dma_engine_mask=mask)
+        sent += bin(mask).count("1")
+
+    if p >= 1:
+        w = _w(p)
+        ps = T["ps%d" % p]
+        senders = _arrival_order(p)
+        g.vector.wait_ge(sem["mm%d" % p], 2)
+        for i, j in enumerate(senders):
+            slot = j if j < p else j - 1
+            g.vector.wait_ge(sem["arr%d" % j], bin(topo.mask(T.cores[j], core)).count("1"))
+            if i:
+                g.vector.wait_ge(sem.acc, i)
+            out = T.res[:, 0:w] if i == len(senders) - 1 else ps[:, 0:w]
+            g.vector.tensor_tensor(out, ps[:, 0:w], T.land[:, slot * w:(slot + 1) * w], AluOpType.add).then_inc(sem.acc, 1)
+        g.sync.wait_ge(sem.acc, len(senders))
+        g.sync.dma_start(T.y[:, 0:w], T.res[0:64, 0:w]).then_inc(sem.st, 16)
+        g.scalar.wait_ge(sem.acc, len(senders))
+        g.scalar.dma_start(T.y[:, w:2 * w], T.res[64:128, 0:w]).then_inc(sem.st, 16)
+        g.wait_ge(sem.st, 32)
+    g.wait_ge(sem.sent, sent)

@@ -4,17 +4,59 @@ N = 8
 CB = 64
 HALF = CB // 2
 
+_PLAN = {
+    0: [("D", 2), ("T", 7), ("T", 1), ("D", 5), ("D", 6), ("D", 4), ("D", 3)],
+    1: [("D", 2), ("D", 5), ("D", 4), ("D", 6), ("D", 3), ("M", 7)],
+    2: [("D", 1), ("T", 7), ("D", 4), ("T", 3), ("D", 5), ("M", 6)],
+    3: [("D", 1), ("T", 6), ("T", 2), ("D", 5), ("D", 4), ("M", 7)],
+    4: [("D", 1), ("D", 7), ("D", 2), ("D", 3), ("D", 5), ("D", 6)],
+    5: [("D", 1), ("D", 6), ("D", 7), ("D", 4), ("D", 2), ("D", 3)],
+    6: [("D", 1), ("D", 4), ("D", 2), ("D", 3), ("D", 7), ("D", 5)],
+    7: [("D", 1), ("D", 3), ("D", 5), ("D", 4), ("D", 2), ("D", 6)],
+}
+
 
 def _w(r):
     return HALF * r
 
 
-_OFF = [sum(_w(q) for q in range(r)) for r in range(N + 1)]
+def _calls(j):
+    out = []
+    for kind, r in _PLAN[j]:
+        if kind == "T" and out and out[-1][0] == "T":
+            out[-1][1].append(r)
+        else:
+            out.append((kind, [r]))
+    return out
+
+
+def _soff(j):
+    off, c = {}, 0
+    for _, r in _PLAN[j]:
+        off[r] = c
+        c += _w(r)
+    return off
+
+
+def _tmap(j):
+    m, c, n = {}, 0, 0
+    for kind, rs in _calls(j):
+        if kind == "T":
+            for r in rs:
+                m[r] = (n, c)
+                c += _w(r)
+            n += 1
+    return m
+
+
+_TW = max(sum(_w(r) for k, r in _PLAN[j] if k == "T") for j in range(N))
+_TN = max(len([1 for k, _ in _calls(j) if k == "T"]) for j in range(N))
 
 SCRATCH = {
     "xs": ("sbuf", [128, N * CB], "float32"),
-    "snd": ("sbuf", [128, _OFF[N]], "float32"),
+    "snd": ("sbuf", [128, sum(_w(r) for r in range(N))], "float32"),
     "land": ("sbuf", [128, (N - 1) * _w(N - 1)], "float32"),
+    "mland": ("sbuf", [128, _TW], "float32"),
     "res": ("sbuf", [128, _w(N - 1)], "float32"),
 }
 for _r in range(1, N):
@@ -23,31 +65,26 @@ for _r in range(1, N):
 SEMAPHORES = (["lda", "ldb", "acc", "sent", "st"]
               + ["mm%d" % r for r in range(1, N)]
               + ["ev%d" % r for r in range(1, N)]
-              + ["arr%d" % j for j in range(N)])
-
-_FIRST = {0: 7, 1: 6, 2: 5, 3: 4, 4: 3, 5: 2, 6: 4, 7: 6}
-
-
-def _order(j):
-    dests = [r for r in range(1, N) if r != j]
-    opener = dests[0]
-    ring = list(range(N - 1, 1, -1))
-    k = ring.index(_FIRST[j])
-    ring = ring[k:] + ring[:k]
-    return [opener] + [r for r in ring if r != j and r != opener]
+              + ["arr%d" % j for j in range(N)]
+              + ["mt%d" % n for n in range(_TN)])
 
 
-def _arrival_order(r):
-    when = {}
-    for j in range(N):
-        if j == r:
-            continue
-        t = 0
-        for d in _order(j):
-            t += 4 + d
-            if d == r:
-                break
-        when[j] = t
+def _arrival_order(r, mate):
+    landed, when = {}, {}
+    for _ in range(3):
+        for j in range(N):
+            t = 0
+            for kind, rs in _calls(j):
+                if kind == "M":
+                    t = max(t, landed.get((mate[j], rs[0]), 0))
+                t += 2 + sum(rs)
+                if kind == "T":
+                    for d in rs:
+                        landed[(j, d)] = t + 9
+                    if r in rs and mate[j] == r:
+                        when[j] = t
+                elif rs[0] == r:
+                    when[j] = t
     return sorted(when, key=lambda j: (when[j], j))
 
 
@@ -56,14 +93,23 @@ def rank_program(g, core, T, topo):
     if p is None:
         return
     sem = T.sem
-    order = _order(p)
-    ca = CB * (order[0] + 1)
+    cores = T.cores
+    mate = {j: k for j in range(N) for k in range(N) if topo.mates(cores[j], cores[k])}
+    for j in range(N):
+        for kind, r in _PLAN[j]:
+            assert kind != "T" or r == mate[j] or (topo.same_plane(cores[mate[j]], cores[r]) and ("M", r) in _PLAN[mate[j]])
+
+    def engines(src, dst):
+        return bin(topo.mask(cores[src], cores[dst])).count("1")
+
+    soff = _soff(p)
+    work = [r for _, r in _PLAN[p]] + ([p] if p >= 1 else [])
+    ca = CB * (work[0] + 1)
 
     g.sync.dma_start(T.xs[:, 0:ca], T.x[:, 0:ca]).then_inc(sem.lda, 16)
     g.scalar.dma_start(T.xs[:, ca:N * CB], T.x[:, ca:N * CB]).then_inc(sem.ldb, 16)
 
     g.tensor.wait_ge(sem.lda, 16)
-    work = order + ([p] if p >= 1 else [])
     for i, r in enumerate(work):
         if i == 1:
             g.tensor.wait_ge(sem.ldb, 16)
@@ -74,31 +120,50 @@ def rank_program(g, core, T, topo):
         g.tensor.matmul(ps[64:128, 0:w], lhsT=blk, rhs=T.xs[:, w:2 * w], start=True, stop=True).then_inc(sem["mm%d" % r], 1)
 
     sent = 0
-    for r in order:
-        w = _w(r)
-        g.vector.wait_ge(sem["mm%d" % r], 2)
-        g.vector.tensor_copy(T.snd[:, _OFF[r]:_OFF[r] + w], T["ps%d" % r][:, 0:w]).then_inc(sem["ev%d" % r], 1)
-        dst = T.cores[r]
-        rid, pid = topo.addr(dst, core)
-        mask = topo.mask(core, dst)
-        slot = p if p < r else p - 1
-        g.wait_ge(sem["ev%d" % r], 1)
-        g.remote_dma(out_ap=T.land[:, slot * w:(slot + 1) * w], in_ap=T.snd[:, _OFF[r]:_OFF[r] + w],
-                     remote_sem=sem["arr%d" % p], local_sem=sem.sent, pid=pid, routing_id=rid, dma_engine_mask=mask)
-        sent += bin(mask).count("1")
+    for kind, rs in _calls(p):
+        for r in rs:
+            w = _w(r)
+            out = T.snd[:, soff[r]:soff[r] + w]
+            g.vector.wait_ge(sem["mm%d" % r], 2)
+            if kind == "M":
+                n, c = _tmap(mate[p])[r]
+                g.vector.wait_ge(sem["mt%d" % n], engines(mate[p], p))
+                g.vector.tensor_tensor(out, T["ps%d" % r][:, 0:w], T.mland[:, c:c + w], AluOpType.add).then_inc(sem["ev%d" % r], 1)
+            else:
+                g.vector.tensor_copy(out, T["ps%d" % r][:, 0:w]).then_inc(sem["ev%d" % r], 1)
+            g.wait_ge(sem["ev%d" % r], 1)
+        wide = sum(_w(r) for r in rs)
+        src = T.snd[:, soff[rs[0]]:soff[rs[0]] + wide]
+        if kind == "T":
+            d = mate[p]
+            n, c = _tmap(p)[rs[0]]
+            dst_ap, rsem = T.mland[:, c:c + wide], sem["mt%d" % n]
+        else:
+            d = rs[0]
+            slot = p if p < d else p - 1
+            dst_ap, rsem = T.land[:, slot * wide:(slot + 1) * wide], sem["arr%d" % p]
+        rid, pid = topo.addr(cores[d], core)
+        g.remote_dma(out_ap=dst_ap, in_ap=src, remote_sem=rsem, local_sem=sem.sent, pid=pid, routing_id=rid,
+                     dma_engine_mask=topo.mask(core, cores[d]))
+        sent += engines(p, d)
 
     if p >= 1:
         w = _w(p)
         ps = T["ps%d" % p]
-        senders = _arrival_order(p)
+        senders = _arrival_order(p, mate)
         g.vector.wait_ge(sem["mm%d" % p], 2)
         for i, j in enumerate(senders):
-            slot = j if j < p else j - 1
-            g.vector.wait_ge(sem["arr%d" % j], bin(topo.mask(T.cores[j], core)).count("1"))
+            if ("T", p) in _PLAN[j]:
+                n, c = _tmap(j)[p]
+                piece, asem = T.mland[:, c:c + w], sem["mt%d" % n]
+            else:
+                slot = j if j < p else j - 1
+                piece, asem = T.land[:, slot * w:(slot + 1) * w], sem["arr%d" % j]
+            g.vector.wait_ge(asem, engines(j, p))
             if i:
                 g.vector.wait_ge(sem.acc, i)
             out = T.res[:, 0:w] if i == len(senders) - 1 else ps[:, 0:w]
-            g.vector.tensor_tensor(out, ps[:, 0:w], T.land[:, slot * w:(slot + 1) * w], AluOpType.add).then_inc(sem.acc, 1)
+            g.vector.tensor_tensor(out, ps[:, 0:w], piece, AluOpType.add).then_inc(sem.acc, 1)
         g.sync.wait_ge(sem.acc, len(senders))
         g.sync.dma_start(T.y[:, 0:w], T.res[0:64, 0:w]).then_inc(sem.st, 16)
         g.scalar.wait_ge(sem.acc, len(senders))

from concourse.mybir import AluOpType

N = 8
CB = 64
HALF = CB // 2

_PLAN = {
    0: [("D", 2), ("T", 7), ("T", 1), ("D", 5), ("D", 6), ("D", 4), ("D", 3)],
    1: [("D", 2), ("D", 5), ("D", 4), ("D", 6), ("D", 3), ("M", 7)],
    2: [("D", 1), ("T", 7), ("D", 4), ("T", 3), ("D", 5), ("M", 6)],
    3: [("D", 1), ("T", 6), ("T", 2), ("D", 5), ("D", 4), ("M", 7)],
    4: [("D", 1), ("D", 7), ("D", 2), ("D", 3), ("D", 5), ("D", 6)],
    5: [("D", 1), ("D", 6), ("D", 7), ("D", 4), ("D", 2), ("D", 3)],
    6: [("D", 1), ("D", 4), ("D", 2), ("D", 3), ("D", 7), ("D", 5)],
    7: [("D", 1), ("D", 3), ("D", 5), ("D", 4), ("D", 2), ("D", 6)],
}


def _w(r):
    return HALF * r


def _calls(j):
    out = []
    for kind, r in _PLAN[j]:
        if kind == "T" and out and out[-1][0] == "T":
            out[-1][1].append(r)
        else:
            out.append((kind, [r]))
    return out


def _soff(j):
    off, c = {}, 0
    for _, r in _PLAN[j]:
        off[r] = c
        c += _w(r)
    return off


def _tmap(j):
    m, c, n = {}, 0, 0
    for kind, rs in _calls(j):
        if kind == "T":
            for r in rs:
                m[r] = (n, c)
                c += _w(r)
            n += 1
    return m


_TW = max(sum(_w(r) for k, r in _PLAN[j] if k == "T") for j in range(N))
_TN = max(len([1 for k, _ in _calls(j) if k == "T"]) for j in range(N))

SCRATCH = {
    "xs": ("sbuf", [128, N * CB], "float32"),
    "snd": ("sbuf", [128, sum(_w(r) for r in range(N))], "float32"),
    "land": ("sbuf", [128, (N - 1) * _w(N - 1)], "float32"),
    "mland": ("sbuf", [128, _TW], "float32"),
    "res": ("sbuf", [128, _w(N - 1)], "float32"),
}
for _r in range(1, N):
    SCRATCH["ps%d" % _r] = ("psum", [128, 512], "float32")

SEMAPHORES = (["lda", "ldb", "acc", "sent", "st"]
              + ["mm%d" % r for r in range(1, N)]
              + ["ev%d" % r for r in range(1, N)]
              + ["arr%d" % j for j in range(N)]
              + ["mt%d" % n for n in range(_TN)])


def _arrival_order(r, mate):
    landed, when = {}, {}
    for _ in range(3):
        for j in range(N):
            t = 0
            for kind, rs in _calls(j):
                if kind == "M":
                    t = max(t, landed.get((mate[j], rs[0]), 0))
                t += 2 + sum(rs)
                if kind == "T":
                    for d in rs:
                        landed[(j, d)] = t + 9
                    if r in rs and mate[j] == r:
                        when[j] = t
                elif rs[0] == r:
                    when[j] = t
    return sorted(when, key=lambda j: (when[j], j))


def rank_program(g, core, T, topo):
    p = T.rank_of(core)
    if p is None:
        return
    sem = T.sem
    cores = T.cores
    mate = {j: k for j in range(N) for k in range(N) if topo.mates(cores[j], cores[k])}
    for j in range(N):
        for kind, r in _PLAN[j]:
            assert kind != "T" or r == mate[j] or (topo.same_plane(cores[mate[j]], cores[r]) and ("M", r) in _PLAN[mate[j]])

    def engines(src, dst):
        return bin(topo.mask(cores[src], cores[dst])).count("1")

    soff = _soff(p)
    work = [r for _, r in _PLAN[p]] + ([p] if p >= 1 else [])
    ca = CB * (work[0] + 1)

    g.sync.dma_start(T.xs[:, 0:ca], T.x[:, 0:ca]).then_inc(sem.lda, 16)
    g.scalar.dma_start(T.xs[:, ca:N * CB], T.x[:, ca:N * CB]).then_inc(sem.ldb, 16)

    g.tensor.wait_ge(sem.lda, 16)
    for i, r in enumerate(work):
        if i == 1:
            g.tensor.wait_ge(sem.ldb, 16)
        w = _w(r)
        ps = T["ps%d" % r]
        blk = T.xs[:, CB * r:CB * r + CB]
        g.tensor.matmul(ps[0:64, 0:w], lhsT=blk, rhs=T.xs[:, 0:w], start=True, stop=True).then_inc(sem["mm%d" % r], 1)
        g.tensor.matmul(ps[64:128, 0:w], lhsT=blk, rhs=T.xs[:, w:2 * w], start=True, stop=True).then_inc(sem["mm%d" % r], 1)

    sent = 0
    for kind, rs in _calls(p):
        for r in rs:
            w = _w(r)
            out = T.snd[:, soff[r]:soff[r] + w]
            g.vector.wait_ge(sem["mm%d" % r], 2)
            if kind == "M":
                n, c = _tmap(mate[p])[r]
                g.vector.wait_ge(sem["mt%d" % n], engines(mate[p], p))
                g.vector.tensor_tensor(out, T["ps%d" % r][:, 0:w], T.mland[:, c:c + w], AluOpType.add).then_inc(sem["ev%d" % r], 1)
            else:
                g.vector.tensor_copy(out, T["ps%d" % r][:, 0:w]).then_inc(sem["ev%d" % r], 1)
            g.wait_ge(sem["ev%d" % r], 1)
        wide = sum(_w(r) for r in rs)
        src = T.snd[:, soff[rs[0]]:soff[rs[0]] + wide]
        if kind == "T":
            d = mate[p]
            n, c = _tmap(p)[rs[0]]
            dst_ap, rsem = T.mland[:, c:c + wide], sem["mt%d" % n]
        else:
            d = rs[0]
            slot = p if p < d else p - 1
            dst_ap, rsem = T.land[:, slot * wide:(slot + 1) * wide], sem["arr%d" % p]
        rid, pid = topo.addr(cores[d], core)
        g.remote_dma(out_ap=dst_ap, in_ap=src, remote_sem=rsem, local_sem=sem.sent, pid=pid, routing_id=rid,
                     dma_engine_mask=topo.mask(core, cores[d]))
        sent += engines(p, d)

    if p >= 1:
        w = _w(p)
        ps = T["ps%d" % p]
        senders = _arrival_order(p, mate)
        g.vector.wait_ge(sem["mm%d" % p], 2)
        for i, j in enumerate(senders):
            if ("T", p) in _PLAN[j]:
                n, c = _tmap(j)[p]
                piece, asem = T.mland[:, c:c + w], sem["mt%d" % n]
            else:
                slot = j if j < p else j - 1
                piece, asem = T.land[:, slot * w:(slot + 1) * w], sem["arr%d" % j]
            g.vector.wait_ge(asem, engines(j, p))
            if i:
                g.vector.wait_ge(sem.acc, i)
            out = T.res[:, 0:w] if i == len(senders) - 1 else ps[:, 0:w]
            g.vector.tensor_tensor(out, ps[:, 0:w], piece, AluOpType.add).then_inc(sem.acc, 1)
        g.sync.wait_ge(sem.acc, len(senders))
        g.sync.dma_start(T.y[:, 0:w], T.res[0:64, 0:w]).then_inc(sem.st, 16)
        g.scalar.wait_ge(sem.acc, len(senders))
        g.scalar.dma_start(T.y[:, w:2 * w], T.res[64:128, 0:w]).then_inc(sem.st, 16)
        g.wait_ge(sem.st, 32)
    g.wait_ge(sem.sent, sent)
